import numpy as np
import ml_dtypes


def mxq(x, axis, fmt="e4m3"):
    dtype, down = {"e4m3": (ml_dtypes.float8_e4m3fn, 7), "e5m2": (ml_dtypes.float8_e5m2, 14)}[fmt]
    v = np.moveaxis(np.asarray(x, np.float32).astype(ml_dtypes.bfloat16).astype(np.float64), axis, -1)
    blocks = v.reshape(v.shape[:-1] + (-1, 32))
    amax = np.abs(blocks).max(-1, keepdims=True)
    byte = np.maximum(np.where(amax > 0, np.frexp(amax)[1] - 1 + 127, 0) - down, 1)
    scale = np.exp2(byte - 127.0)
    codes = (blocks / scale).astype(np.float32).astype(dtype).astype(np.float64)
    return np.moveaxis((codes * scale).reshape(v.shape), -1, axis)


WIDE = False


def mx_kscale(k):
    if not WIDE:
        return np.ones(k)
    levels = np.array([10, -10, 5, -5, 0])
    if k % 512:
        return np.exp2(np.random.permutation(np.resize(levels, k // 32))).repeat(32)
    a = np.empty((k // 512, 16))
    for p in range(k // 512):
        a[p, :8] = np.random.permutation(np.resize(levels, 8))
        for g in range(8):
            far = levels[np.abs(levels - a[p, g]) >= 10]
            a[p, g + 8] = far[np.random.randint(len(far))]
    return np.exp2(a.ravel()).repeat(32)


def f64(x):
    return np.asarray(x).astype(np.float64)


def striped(idx):
    return np.tile(idx.reshape(-1, 16).T, (8, 1)).astype(np.uint16)


def unstriped(offs):
    return offs[:16].T.reshape(-1).astype(np.int64)


def pack_weight(w):
    k, n = w.shape
    w = f64(np.asarray(w, np.float32).astype(ml_dtypes.bfloat16)).reshape(k // 32, 32, n)
    amax = np.abs(w).max(1)
    byte = np.clip(np.where(amax > 0, np.frexp(amax)[1] - 1 + 127 - 7, 1), 1, 254)
    scaled = (w * np.exp2(127.0 - byte)[:, None, :]).reshape(k, n).astype(np.float32)
    words = np.ascontiguousarray(scaled.reshape(k // 512, 128, 4, n).transpose(0, 1, 3, 2)).astype(ml_dtypes.float8_e4m3fn).view(np.uint8)
    return words, np.ascontiguousarray(byte.astype(np.uint8).reshape(k // 512, 16, n))


def unpack_weight(words, scales):
    g, p, n, _ = words.shape
    vals = np.ascontiguousarray(words).view(ml_dtypes.float8_e4m3fn).astype(np.float64) * np.repeat(np.exp2(scales.astype(np.float64) - 127.0), 8, axis=1)[..., None]
    return vals.transpose(0, 1, 3, 2).reshape(g * 512, n)


def sigmoid(v):
    return 1.0 / (1.0 + np.exp(-np.maximum(v, -700.0)))


K, T, S, H, N = 1024, 1024, 512, 512, 128


def setup_inputs():
    n = np.random.standard_normal
    s = mx_kscale(K)[:, None]
    u = mx_kscale(H)
    packed_xT = pack_weight(n((K, T)) * s)
    return {
        "x_words": packed_xT[0],
        "x_scales": packed_xT[1],
        "w1": (n((K, H)) / np.sqrt(K) / s).astype(np.float32),
        "geno": (np.floor(np.random.uniform(0.0, 2.999, (H, S)))).astype(np.float32),
        "unit": (np.random.uniform(0.5, 1.5, (H, 1)) * u[:, None]).astype(np.float32),
        "fk": (np.random.uniform(0.0, 2.0, (H, N)) / H / u[:, None]).astype(np.float32),
        "fc": (np.random.uniform(0.0, 2.0, (H, N)) / H / u[:, None]).astype(np.float32),
        "frac": (np.random.uniform(0.0, 1.0, (N, S)) ** 2).astype(np.float32),
        "offs": striped(np.random.permutation(T)[:S]),
    }


def reference(x_words, x_scales, w1, geno, unit, fk, fc, frac, offs):
    xq = unpack_weight(x_words, x_scales)[:, unstriped(offs)]
    freq = 0.9 * (sigmoid(mxq(f64(w1), 0, "e4m3").T @ xq)) + 0.05
    a = f64(unit) * (f64(geno) / freq)
    e1 = f64(unit) * ((-1.0 * f64(geno) + 2.0) / (-1.0 * freq + 1.0))
    rr = mxq(f64(fk), 0, "e4m3").T @ mxq(a, 0, "e4m3") + mxq(f64(fc), 0, "e4m3").T @ mxq(e1, 0, "e4m3")
    return f64(frac) * rr

@@ -1,0 +1,214 @@
+import math
+from contextlib import ExitStack
+
+import concourse.mybir as mybir
+
+K, T, S, H, N = 1024, 1024, 512, 512, 128
+FLOPS = 2 * K * H * S + 2 * 2 * H * N * S
+
+F32 = mybir.dt.float32
+BF16 = mybir.dt.bfloat16
+I32 = mybir.dt.int32
+U32 = mybir.dt.uint32
+U16 = mybir.dt.uint16
+U8 = mybir.dt.uint8
+FP8X4 = mybir.dt.float8_e4m3fn_x4
+ACT = mybir.ActivationFunctionType
+ALU = mybir.AluOpType
+
+P = 128
+PACK = 4
+PASSES = K // (P * PACK)
+CHUNK = 128
+CHUNKS = S // CHUNK
+HALF = S // 2
+LN19 = math.log(19.0)
+
+
+def tile_picked_yadmix_em_p_kernel(tc, x_words, x_scales, w1, geno, unit, fk, fc, frac, offs, out):
+    nc = tc.nc
+    with ExitStack() as ctx:
+        keep = ctx.enter_context(tc.tile_pool(name="keep", bufs=1))
+        psum = ctx.enter_context(tc.psum_pool(name="psum", bufs=1))
+
+        def tile(shape, dtype, name):
+            return keep.tile(shape, dtype, name=name, align_bytes=64)
+
+        offsets = keep.tile([P, S // 16], U16, name="offsets")
+        nc.sync.dma_start(offsets[:], offs)
+
+        x_plane = tile([P, T], U8, "x_plane")
+        nc.gpsimd.memset(x_plane[:].bitcast(I32), 0)
+        for q in range(4):
+            (nc.gpsimd if q < 2 else nc.scalar).dma_start(x_plane[32 * q : 32 * q + 4 * PASSES, :].bitcast(I32), x_scales[:, 4 * q : 4 * q + 4, :].bitcast(I32))
+        warm = tile([P, 1], F32, "warm")
+        warm_out = tile([P, 1], F32, "warm_out")
+        nc.gpsimd.memset(warm[:], 0.0)
+        nc.scalar.activation(warm_out[:], warm[:], ACT.Sigmoid)
+        x_table = [tile([P, T], U32, f"x_table{o}") for o in range(PASSES)]
+
+        def load_x(o):
+            nc.sync.dma_start(x_table[o][:].bitcast(I32), x_words[o].rearrange("p n t -> p (n t)").bitcast(I32))
+
+        def load_w(o, h):
+            raw = tile([P, PACK, H // 2], F32, f"w_raw{o}_{h}")
+            nc.sync.dma_start(raw[:], w1[512 * o : 512 * (o + 1), h * H // 2 : (h + 1) * H // 2].rearrange("(p j) c -> p j c", j=PACK))
+            return raw
+
+        def load_geno(h):
+            g = tile([P, PACK, HALF], F32, f"geno{h}")
+            nc.sync.dma_start(g[:], geno[:, h * HALF : (h + 1) * HALF].rearrange("(p t) n -> p t n", t=PACK))
+            return g
+
+        unit_sb = tile([P, PACK], F32, "unit_sb")
+        nc.scalar.dma_start(unit_sb[:], unit.rearrange("(p t) o -> p (t o)", t=PACK))
+        load_x(0)
+        w_raw = {(0, 0): load_w(0, 0)}
+        geno_sb = [load_geno(0)]
+        w_raw[0, 1] = load_w(0, 1)
+        w_raw[1, 0] = load_w(1, 0)
+        w_raw[1, 1] = load_w(1, 1)
+        load_x(1)
+        geno_sb.append(load_geno(1))
+        f_raw = []
+        for name, f in (("fk", fk), ("fc", fc)):
+            raw = tile([P, PACK, N], F32, f"{name}_raw")
+            nc.sync.dma_start(raw[:], f.rearrange("(p j) n -> p j n", j=PACK))
+            f_raw.append(raw)
+        frac_sb = tile([P, S], F32, "frac_sb")
+        nc.sync.dma_start(frac_sb[:], frac)
+
+        gain = tile([P, PACK], F32, "gain")
+        gain_neg = tile([P, PACK], F32, "gain_neg")
+        gain_two = tile([P, PACK], F32, "gain_two")
+        for dst, factor in ((gain, 1.0), (gain_neg, -1.0), (gain_two, 2.0)):
+            nc.gpsimd.tensor_scalar(dst[:], unit_sb[:], factor * 360.0 / 19.0, 0.0, ALU.mult, ALU.add)
+
+        picked0 = tile([P, S], U32, "picked0")
+        nc.vector.tensor_copy(picked0[:], x_table[0][:].indirect(offsets[:]))
+        picked_plane = tile([P, S], U8, "picked_plane")
+        nc.vector.tensor_copy(picked_plane[:], x_plane[:].indirect(offsets[:]))
+
+        g_a = [tile([P, PACK, HALF], F32, f"g_a{h}") for h in range(2)]
+        g_e = [tile([P, PACK, HALF], F32, f"g_e{h}") for h in range(2)]
+
+        def scale_geno(h, on_scalar):
+            for i in range(2):
+                for t in range(PACK):
+                    col = slice(t, t + 1)
+                    src = geno_sb[h][:, t, :]
+                    if PACK * i + t < on_scalar:
+                        if i == 0:
+                            nc.scalar.activation(g_a[h][:, t, :], src, ACT.Copy, scale=gain[:, col])
+                        else:
+                            nc.scalar.activation(g_e[h][:, t, :], src, ACT.Identity, scale=gain_neg[:, col], bias=gain_two[:, col])
+                    elif i == 0:
+                        nc.vector.tensor_scalar(g_a[h][:, t, :], src, gain[:, col], None, ALU.mult)
+                    else:
+                        nc.vector.tensor_scalar(g_e[h][:, t, :], src, gain_neg[:, col], gain_two[:, col], ALU.mult, ALU.add)
+
+        w_bf = [tile([P, PACK, P, PACK], BF16, f"w_bf{o}") for o in range(PASSES)]
+        w_codes = [tile([P, H], U32, f"w_codes{o}") for o in range(PASSES)]
+        w_plane = [tile([P, H], U8, f"w_plane{o}") for o in range(PASSES)]
+        for (o, h), raw in w_raw.items():
+            ms = P // 2
+            m0 = h * ms
+            src = raw[:].rearrange("p j (m t) -> p m j t", t=PACK)
+            dst = w_bf[o][:].rearrange("p t m j -> p m j t")
+            share = ms if (o, h) == (0, 0) else 24
+            nc.scalar.copy(dst[:, m0 : m0 + share], src[:, 0:share])
+            if share < ms:
+                nc.vector.tensor_copy(dst[:, m0 + share : m0 + ms], src[:, share:ms])
+            if (o, h) == (0, 0):
+                scale_geno(0, 4)
+            if h == 1:
+                nc.vector.quantize_mx(out=w_codes[o][:].bitcast(FP8X4), scales=w_plane[o][:], in_=w_bf[o][:].rearrange("p t m j -> p (t m j)"))
+
+        hidden = {}
+
+        def look_up(first, count, tag):
+            words = keep.tile([P, count * CHUNK], U32, name=f"picked1_{first}", tag=tag, align_bytes=64)
+            nc.vector.tensor_copy(words[:], x_table[1][:].indirect(offsets[:, first * CHUNK // 16 : (first + count) * CHUNK // 16]))
+            return words
+
+        def first_product(c, words):
+            cols = slice(c * CHUNK, (c + 1) * CHUNK)
+            acc = psum.tile([P, PACK, CHUNK], F32, name=f"hidden{c}", tag="hidden", bufs=2)
+            for t in range(PACK):
+                m_cols = slice(t * P, (t + 1) * P)
+                for o in range(PASSES):
+                    rhs = picked0[:, cols] if o == 0 else words
+                    nc.tensor.matmul_mx(
+                        out=acc[:, t, :],
+                        lhsT=w_codes[o][:, m_cols].bitcast(FP8X4),
+                        lhsT_scale=w_plane[o][:, m_cols],
+                        rhs=rhs.bitcast(FP8X4),
+                        rhs_scale=picked_plane[4 * o : P, cols],
+                        start=(o == 0),
+                        stop=(o == PASSES - 1),
+                    )
+            hidden[c] = acc
+
+        f_bf = tile([P, 2, N, PACK], BF16, "f_bf")
+        f_codes = tile([P, 2 * N], U32, "f_codes")
+        f_plane = tile([P, 2 * N], U8, "f_plane")
+
+        def quantise_f():
+            for i in range(2):
+                nc.scalar.copy(f_bf[:, i], f_raw[i][:].rearrange("p j n -> p n j"))
+            nc.vector.quantize_mx(out=f_codes[:].bitcast(FP8X4), scales=f_plane[:], in_=f_bf[:].rearrange("p i n j -> p (i n j)"))
+
+        ae_bf = [tile([P, 2, CHUNK * PACK], BF16, f"ae_bf{c}") for c in range(CHUNKS)]
+        ae_codes = [tile([P, 2 * CHUNK], U32, f"ae_codes{c}") for c in range(CHUNKS)]
+        ae_plane = [tile([P, 2 * CHUNK], U8, f"ae_plane{c}") for c in range(CHUNKS)]
+
+        def elementwise(c):
+            h, within = divmod(c * CHUNK, HALF)
+            cols = slice(within, within + CHUNK)
+            for i, (sign, g) in enumerate(((-1.0, g_a[h]), (1.0, g_e[h]))):
+                sig = tile([P, CHUNK, PACK], F32, f"sig{c}_{i}")
+                nc.scalar.activation(sig[:], hidden[c][:].rearrange("p t n -> p n t"), ACT.Sigmoid, bias=-LN19, scale=sign)
+                nc.vector.scalar_tensor_tensor(
+                    ae_bf[c][:, i, :].rearrange("p (n t) -> p n t", t=PACK), sig[:], 1.0 / 18.0,
+                    g[:, :, cols].rearrange("p t n -> p n t"), ALU.add, ALU.mult,
+                )
+
+        def quantise_ae(c):
+            nc.vector.quantize_mx(out=ae_codes[c][:].bitcast(FP8X4), scales=ae_plane[c][:], in_=ae_bf[c][:].rearrange("p i w -> p (i w)"))
+
+        def finish(first, count):
+            cols = slice(first * CHUNK, (first + count) * CHUNK)
+            acc = psum.tile([P, count * CHUNK], F32, name=f"rr{first}")
+            for c in range(first, first + count):
+                for i in range(2):
+                    nc.tensor.matmul_mx(
+                        out=acc[:, (c - first) * CHUNK : (c - first + 1) * CHUNK],
+                        lhsT=f_codes[:, i * N : (i + 1) * N].bitcast(FP8X4),
+                        lhsT_scale=f_plane[:, i * N : (i + 1) * N],
+                        rhs=ae_codes[c][:, i * CHUNK : (i + 1) * CHUNK].bitcast(FP8X4),
+                        rhs_scale=ae_plane[c][:, i * CHUNK : (i + 1) * CHUNK],
+                        start=(i == 0),
+                        stop=(i == 1),
+                    )
+            result = tile([P, count * CHUNK], F32, f"result{first}")
+            nc.vector.tensor_tensor(result[:], acc[:], frac_sb[:, cols], ALU.mult)
+            nc.sync.dma_start(out[:, cols], result[:])
+
+        first_product(0, look_up(0, 1, "early")[:])
+        late = look_up(2, 2, "late")
+        first_product(1, look_up(1, 1, "early")[:])
+        elementwise(0)
+        scale_geno(1, 3)
+        first_product(2, late[:, 0:CHUNK])
+        elementwise(1)
+        first_product(3, late[:, CHUNK : 2 * CHUNK])
+        quantise_ae(0)
+        quantise_ae(1)
+        quantise_f()
+        elementwise(2)
+        finish(0, 2)
+        elementwise(3)
+        quantise_ae(2)
+        quantise_ae(3)
+        finish(2, 1)
+        finish(3, 1)

@@ -34,42 +34,45 @@ def tile_picked_yadmix_em_p_kernel(tc, x_words, x_scales, w1, geno, unit, fk, fc
         def tile(shape, dtype, name):
             return keep.tile(shape, dtype, name=name, align_bytes=64)
 
-        offsets = keep.tile([P, S // 16], U16, name="offsets")
-        nc.sync.dma_start(offsets[:], offs)
-
-        x_plane = tile([P, T], U8, "x_plane")
-        nc.gpsimd.memset(x_plane[:].bitcast(I32), 0)
-        for q in range(4):
-            (nc.gpsimd if q < 2 else nc.scalar).dma_start(x_plane[32 * q : 32 * q + 4 * PASSES, :].bitcast(I32), x_scales[:, 4 * q : 4 * q + 4, :].bitcast(I32))
-        warm = tile([P, 1], F32, "warm")
-        warm_out = tile([P, 1], F32, "warm_out")
-        nc.gpsimd.memset(warm[:], 0.0)
-        nc.scalar.activation(warm_out[:], warm[:], ACT.Sigmoid)
         x_table = [tile([P, T], U32, f"x_table{o}") for o in range(PASSES)]
 
         def load_x(o):
             nc.sync.dma_start(x_table[o][:].bitcast(I32), x_words[o].rearrange("p n t -> p (n t)").bitcast(I32))
 
-        def load_w(o, h):
-            raw = tile([P, PACK, H // 2], F32, f"w_raw{o}_{h}")
-            nc.sync.dma_start(raw[:], w1[512 * o : 512 * (o + 1), h * H // 2 : (h + 1) * H // 2].rearrange("(p j) c -> p j c", j=PACK))
-            return raw
+        def load_w(o, c0, width):
+            raw = tile([P, PACK, width], F32, f"w_raw{o}_{c0}")
+            nc.sync.dma_start(raw[:], w1[512 * o : 512 * (o + 1), c0 : c0 + width].rearrange("(p j) c -> p j c", j=PACK))
+            return o, c0, width, raw
 
         def load_geno(h):
-            g = tile([P, PACK, HALF], F32, f"geno{h}")
-            nc.sync.dma_start(g[:], geno[:, h * HALF : (h + 1) * HALF].rearrange("(p t) n -> p t n", t=PACK))
+            g = tile([P, 2, S], F32, f"geno{h}")
+            nc.sync.dma_start(g[:], geno.rearrange("(p t) n -> p t n", t=PACK)[:, 2 * h : 2 * h + 2, :])
             return g
 
+        w_raw = [load_w(0, 0, H // 2)]
+        offsets = keep.tile([P, S // 16], U16, name="offsets")
+        nc.sync.dma_start(offsets[:], offs)
+
+        x_rows = tile([P, T], U8, "x_rows")
+        x_plane = tile([P, T], U8, "x_plane")
+        nc.gpsimd.memset(x_plane[:].bitcast(I32), 0)
+        for q in range(4):
+            live = slice(32 * q, 32 * q + 4 * PASSES)
+            nc.sync.dma_start(x_rows[live, :].bitcast(I32), x_scales[:, 4 * q : 4 * q + 4, :].bitcast(I32))
+            nc.vector.tensor_copy(x_plane[live, :].bitcast(I32), x_rows[live, :].bitcast(I32))
+        warm = tile([P, 1], F32, "warm")
+        warm_out = tile([P, 1], F32, "warm_out")
+        nc.gpsimd.memset(warm[:], 0.0)
+        nc.scalar.activation(warm_out[:], warm[:], ACT.Sigmoid)
+
         unit_sb = tile([P, PACK], F32, "unit_sb")
-        nc.scalar.dma_start(unit_sb[:], unit.rearrange("(p t) o -> p (t o)", t=PACK))
         load_x(0)
-        w_raw = {(0, 0): load_w(0, 0)}
-        geno_sb = [load_geno(0)]
-        w_raw[0, 1] = load_w(0, 1)
-        w_raw[1, 0] = load_w(1, 0)
-        w_raw[1, 1] = load_w(1, 1)
+        w_raw.append(load_w(0, H // 2, H // 2))
+        nc.sync.dma_start(unit_sb[:], unit.rearrange("(p t) o -> p (t o)", t=PACK))
+        w_raw.append(load_w(1, 0, H // 2))
+        w_raw.append(load_w(1, H // 2, H // 2))
         load_x(1)
-        geno_sb.append(load_geno(1))
+        geno_sb = [load_geno(0), load_geno(1)]
         f_raw = []
         for name, f in (("fk", fk), ("fc", fc)):
             raw = tile([P, PACK, N], F32, f"{name}_raw")
@@ -89,39 +92,33 @@ def tile_picked_yadmix_em_p_kernel(tc, x_words, x_scales, w1, geno, unit, fk, fc
         picked_plane = tile([P, S], U8, "picked_plane")
         nc.vector.tensor_copy(picked_plane[:], x_plane[:].indirect(offsets[:]))
 
-        g_a = [tile([P, PACK, HALF], F32, f"g_a{h}") for h in range(2)]
-        g_e = [tile([P, PACK, HALF], F32, f"g_e{h}") for h in range(2)]
+        g_a = tile([P, PACK, S], F32, "g_a")
+        g_e = tile([P, PACK, S], F32, "g_e")
 
-        def scale_geno(h, on_scalar):
-            for i in range(2):
-                for t in range(PACK):
-                    col = slice(t, t + 1)
-                    src = geno_sb[h][:, t, :]
-                    if PACK * i + t < on_scalar:
-                        if i == 0:
-                            nc.scalar.activation(g_a[h][:, t, :], src, ACT.Copy, scale=gain[:, col])
-                        else:
-                            nc.scalar.activation(g_e[h][:, t, :], src, ACT.Identity, scale=gain_neg[:, col], bias=gain_two[:, col])
-                    elif i == 0:
-                        nc.vector.tensor_scalar(g_a[h][:, t, :], src, gain[:, col], None, ALU.mult)
-                    else:
-                        nc.vector.tensor_scalar(g_e[h][:, t, :], src, gain_neg[:, col], gain_two[:, col], ALU.mult, ALU.add)
+        def scale_geno():
+            for t in range(PACK):
+                col = slice(t, t + 1)
+                src = geno_sb[t // 2][:, t % 2, :]
+                if t == 0:
+                    nc.scalar.activation(g_a[:, t, :], src, ACT.Copy, scale=gain[:, col])
+                    nc.scalar.activation(g_e[:, t, :], src, ACT.Identity, scale=gain_neg[:, col], bias=gain_two[:, col])
+                else:
+                    nc.vector.tensor_scalar(g_a[:, t, :], src, gain[:, col], None, ALU.mult)
+                    nc.vector.tensor_scalar(g_e[:, t, :], src, gain_neg[:, col], gain_two[:, col], ALU.mult, ALU.add)
 
         w_bf = [tile([P, PACK, P, PACK], BF16, f"w_bf{o}") for o in range(PASSES)]
         w_codes = [tile([P, H], U32, f"w_codes{o}") for o in range(PASSES)]
         w_plane = [tile([P, H], U8, f"w_plane{o}") for o in range(PASSES)]
-        for (o, h), raw in w_raw.items():
-            ms = P // 2
-            m0 = h * ms
+        for o, c0, width, raw in w_raw:
+            ms = width // PACK
+            m0 = c0 // PACK
             src = raw[:].rearrange("p j (m t) -> p m j t", t=PACK)
             dst = w_bf[o][:].rearrange("p t m j -> p m j t")
-            share = ms if (o, h) == (0, 0) else 24
+            share = ms * 3 // 8 if (o, c0) == (1, H // 2) else ms
             nc.scalar.copy(dst[:, m0 : m0 + share], src[:, 0:share])
             if share < ms:
                 nc.vector.tensor_copy(dst[:, m0 + share : m0 + ms], src[:, share:ms])
-            if (o, h) == (0, 0):
-                scale_geno(0, 4)
-            if h == 1:
+            if c0 + width == H:
                 nc.vector.quantize_mx(out=w_codes[o][:].bitcast(FP8X4), scales=w_plane[o][:], in_=w_bf[o][:].rearrange("p t m j -> p (t m j)"))
 
         hidden = {}
@@ -163,13 +160,15 @@ def tile_picked_yadmix_em_p_kernel(tc, x_words, x_scales, w1, geno, unit, fk, fc
         ae_plane = [tile([P, 2 * CHUNK], U8, f"ae_plane{c}") for c in range(CHUNKS)]
 
         def elementwise(c):
-            h, within = divmod(c * CHUNK, HALF)
-            cols = slice(within, within + CHUNK)
-            for i, (sign, g) in enumerate(((-1.0, g_a[h]), (1.0, g_e[h]))):
-                sig = tile([P, CHUNK, PACK], F32, f"sig{c}_{i}")
-                nc.scalar.activation(sig[:], hidden[c][:].rearrange("p t n -> p n t"), ACT.Sigmoid, bias=-LN19, scale=sign)
+            cols = slice(c * CHUNK, (c + 1) * CHUNK)
+            for i, (sign, g) in enumerate(((-1.0, g_a), (1.0, g_e))):
+                if c == 0:
+                    sig = geno_sb[0][:, i, :].rearrange("p (n t) -> p n t", t=PACK)
+                else:
+                    sig = tile([P, CHUNK, PACK], F32, f"sig{c}_{i}")[:]
+                nc.scalar.activation(sig, hidden[c][:].rearrange("p t n -> p n t"), ACT.Sigmoid, bias=-LN19, scale=sign)
                 nc.vector.scalar_tensor_tensor(
-                    ae_bf[c][:, i, :].rearrange("p (n t) -> p n t", t=PACK), sig[:], 1.0 / 18.0,
+                    ae_bf[c][:, i, :].rearrange("p (n t) -> p n t", t=PACK), sig, 1.0 / 18.0,
                     g[:, :, cols].rearrange("p t n -> p n t"), ALU.add, ALU.mult,
                 )
 
@@ -194,11 +193,12 @@ def tile_picked_yadmix_em_p_kernel(tc, x_words, x_scales, w1, geno, unit, fk, fc
             nc.vector.tensor_tensor(result[:], acc[:], frac_sb[:, cols], ALU.mult)
             nc.sync.dma_start(out[:, cols], result[:])
 
-        first_product(0, look_up(0, 1, "early")[:])
+        early = look_up(0, 2, "early")
+        first_product(0, early[:, 0:CHUNK])
+        first_product(1, early[:, CHUNK : 2 * CHUNK])
         late = look_up(2, 2, "late")
-        first_product(1, look_up(1, 1, "early")[:])
+        scale_geno()
         elementwise(0)
-        scale_geno(1, 3)
         first_product(2, late[:, 0:CHUNK])
         elementwise(1)
         first_product(3, late[:, CHUNK : 2 * CHUNK])

@@ -152,7 +152,7 @@ def tile_picked_yadmix_em_p_kernel(tc, x_words, x_scales, w1, geno, unit, fk, fc
 
         def quantise_f():
             for i in range(2):
-                nc.scalar.copy(f_bf[:, i], f_raw[i][:].rearrange("p j n -> p n j"))
+                nc.scalar.copy(f_bf[:, i].rearrange("p (n q) j -> p n j q", q=4), f_raw[i][:].rearrange("p j (n q) -> p n j q", q=4))
             nc.vector.quantize_mx(out=f_codes[:].bitcast(FP8X4), scales=f_plane[:], in_=f_bf[:].rearrange("p i n j -> p (i n j)"))
 
         ae_bf = [tile([P, 2, CHUNK * PACK], BF16, f"ae_bf{c}") for c in range(CHUNKS)]
@@ -206,9 +206,9 @@ def tile_picked_yadmix_em_p_kernel(tc, x_words, x_scales, w1, geno, unit, fk, fc
         quantise_ae(1)
         quantise_f()
         elementwise(2)
-        finish(0, 2)
         elementwise(3)
         quantise_ae(2)
         quantise_ae(3)
+        finish(0, 2)
         finish(2, 1)
         finish(3, 1)

import math
from contextlib import ExitStack

import concourse.mybir as mybir

K, T, S, H, N = 1024, 1024, 512, 512, 128
FLOPS = 2 * K * H * S + 2 * 2 * H * N * S

F32 = mybir.dt.float32
BF16 = mybir.dt.bfloat16
I32 = mybir.dt.int32
U32 = mybir.dt.uint32
U16 = mybir.dt.uint16
U8 = mybir.dt.uint8
FP8X4 = mybir.dt.float8_e4m3fn_x4
ACT = mybir.ActivationFunctionType
ALU = mybir.AluOpType

P = 128
PACK = 4
PASSES = K // (P * PACK)
CHUNK = 128
CHUNKS = S // CHUNK
HALF = S // 2
LN19 = math.log(19.0)


def tile_picked_yadmix_em_p_kernel(tc, x_words, x_scales, w1, geno, unit, fk, fc, frac, offs, out):
    nc = tc.nc
    with ExitStack() as ctx:
        keep = ctx.enter_context(tc.tile_pool(name="keep", bufs=1))
        psum = ctx.enter_context(tc.psum_pool(name="psum", bufs=1))

        def tile(shape, dtype, name):
            return keep.tile(shape, dtype, name=name, align_bytes=64)

        x_table = [tile([P, T], U32, f"x_table{o}") for o in range(PASSES)]

        def load_x(o):
            nc.sync.dma_start(x_table[o][:].bitcast(I32), x_words[o].rearrange("p n t -> p (n t)").bitcast(I32))

        def load_w(o, c0, width):
            raw = tile([P, PACK, width], F32, f"w_raw{o}_{c0}")
            nc.sync.dma_start(raw[:], w1[512 * o : 512 * (o + 1), c0 : c0 + width].rearrange("(p j) c -> p j c", j=PACK))
            return o, c0, width, raw

        def load_geno(h):
            g = tile([P, 2, S], F32, f"geno{h}")
            nc.sync.dma_start(g[:], geno.rearrange("(p t) n -> p t n", t=PACK)[:, 2 * h : 2 * h + 2, :])
            return g

        w_raw = [load_w(0, 0, H // 2)]
        offsets = keep.tile([P, S // 16], U16, name="offsets")
        nc.sync.dma_start(offsets[:], offs)

        x_rows = tile([P, T], U8, "x_rows")
        x_plane = tile([P, T], U8, "x_plane")
        nc.gpsimd.memset(x_plane[:].bitcast(I32), 0)
        for q in range(4):
            live = slice(32 * q, 32 * q + 4 * PASSES)
            nc.sync.dma_start(x_rows[live, :].bitcast(I32), x_scales[:, 4 * q : 4 * q + 4, :].bitcast(I32))
            nc.vector.tensor_copy(x_plane[live, :].bitcast(I32), x_rows[live, :].bitcast(I32))
        warm = tile([P, 1], F32, "warm")
        warm_out = tile([P, 1], F32, "warm_out")
        nc.gpsimd.memset(warm[:], 0.0)
        nc.scalar.activation(warm_out[:], warm[:], ACT.Sigmoid)

        unit_sb = tile([P, PACK], F32, "unit_sb")
        load_x(0)
        w_raw.append(load_w(0, H // 2, H // 2))
        nc.sync.dma_start(unit_sb[:], unit.rearrange("(p t) o -> p (t o)", t=PACK))
        w_raw.append(load_w(1, 0, H // 2))
        w_raw.append(load_w(1, H // 2, H // 2))
        load_x(1)
        geno_sb = [load_geno(0), load_geno(1)]
        f_raw = []
        for name, f in (("fk", fk), ("fc", fc)):
            raw = tile([P, PACK, N], F32, f"{name}_raw")
            nc.sync.dma_start(raw[:], f.rearrange("(p j) n -> p j n", j=PACK))
            f_raw.append(raw)
        frac_sb = tile([P, S], F32, "frac_sb")
        nc.sync.dma_start(frac_sb[:], frac)

        gain = tile([P, PACK], F32, "gain")
        gain_neg = tile([P, PACK], F32, "gain_neg")
        gain_two = tile([P, PACK], F32, "gain_two")
        for dst, factor in ((gain, 1.0), (gain_neg, -1.0), (gain_two, 2.0)):
            nc.gpsimd.tensor_scalar(dst[:], unit_sb[:], factor * 360.0 / 19.0, 0.0, ALU.mult, ALU.add)

        picked0 = tile([P, S], U32, "picked0")
        nc.vector.tensor_copy(picked0[:], x_table[0][:].indirect(offsets[:]))
        picked_plane = tile([P, S], U8, "picked_plane")
        nc.vector.tensor_copy(picked_plane[:], x_plane[:].indirect(offsets[:]))

        g_a = tile([P, PACK, S], F32, "g_a")
        g_e = tile([P, PACK, S], F32, "g_e")

        def scale_geno():
            for t in range(PACK):
                col = slice(t, t + 1)
                src = geno_sb[t // 2][:, t % 2, :]
                if t == 0:
                    nc.scalar.activation(g_a[:, t, :], src, ACT.Copy, scale=gain[:, col])
                    nc.scalar.activation(g_e[:, t, :], src, ACT.Identity, scale=gain_neg[:, col], bias=gain_two[:, col])
                else:
                    nc.vector.tensor_scalar(g_a[:, t, :], src, gain[:, col], None, ALU.mult)
                    nc.vector.tensor_scalar(g_e[:, t, :], src, gain_neg[:, col], gain_two[:, col], ALU.mult, ALU.add)

        w_bf = [tile([P, PACK, P, PACK], BF16, f"w_bf{o}") for o in range(PASSES)]
        w_codes = [tile([P, H], U32, f"w_codes{o}") for o in range(PASSES)]
        w_plane = [tile([P, H], U8, f"w_plane{o}") for o in range(PASSES)]
        for o, c0, width, raw in w_raw:
            ms = width // PACK
            m0 = c0 // PACK
            src = raw[:].rearrange("p j (m t) -> p m j t", t=PACK)
            dst = w_bf[o][:].rearrange("p t m j -> p m j t")
            share = ms * 3 // 8 if (o, c0) == (1, H // 2) else ms
            nc.scalar.copy(dst[:, m0 : m0 + share], src[:, 0:share])
            if share < ms:
                nc.vector.tensor_copy(dst[:, m0 + share : m0 + ms], src[:, share:ms])
            if c0 + width == H:
                nc.vector.quantize_mx(out=w_codes[o][:].bitcast(FP8X4), scales=w_plane[o][:], in_=w_bf[o][:].rearrange("p t m j -> p (t m j)"))

        hidden = {}

        def look_up(first, count, tag):
            words = keep.tile([P, count * CHUNK], U32, name=f"picked1_{first}", tag=tag, align_bytes=64)
            nc.vector.tensor_copy(words[:], x_table[1][:].indirect(offsets[:, first * CHUNK // 16 : (first + count) * CHUNK // 16]))
            return words

        def first_product(c, words):
            cols = slice(c * CHUNK, (c + 1) * CHUNK)
            acc = psum.tile([P, PACK, CHUNK], F32, name=f"hidden{c}", tag="hidden", bufs=2)
            for t in range(PACK):
                m_cols = slice(t * P, (t + 1) * P)
                for o in range(PASSES):
                    rhs = picked0[:, cols] if o == 0 else words
                    nc.tensor.matmul_mx(
                        out=acc[:, t, :],
                        lhsT=w_codes[o][:, m_cols].bitcast(FP8X4),
                        lhsT_scale=w_plane[o][:, m_cols],
                        rhs=rhs.bitcast(FP8X4),
                        rhs_scale=picked_plane[4 * o : P, cols],
                        start=(o == 0),
                        stop=(o == PASSES - 1),
                    )
            hidden[c] = acc

        f_bf = tile([P, 2, N, PACK], BF16, "f_bf")
        f_codes = tile([P, 2 * N], U32, "f_codes")
        f_plane = tile([P, 2 * N], U8, "f_plane")

        def quantise_f():
            for i in range(2):
                nc.scalar.copy(f_bf[:, i].rearrange("p (n q) j -> p n j q", q=4), f_raw[i][:].rearrange("p j (n q) -> p n j q", q=4))
            nc.vector.quantize_mx(out=f_codes[:].bitcast(FP8X4), scales=f_plane[:], in_=f_bf[:].rearrange("p i n j -> p (i n j)"))

        ae_bf = [tile([P, 2, CHUNK * PACK], BF16, f"ae_bf{c}") for c in range(CHUNKS)]
        ae_codes = [tile([P, 2 * CHUNK], U32, f"ae_codes{c}") for c in range(CHUNKS)]
        ae_plane = [tile([P, 2 * CHUNK], U8, f"ae_plane{c}") for c in range(CHUNKS)]

        def elementwise(c):
            cols = slice(c * CHUNK, (c + 1) * CHUNK)
            for i, (sign, g) in enumerate(((-1.0, g_a), (1.0, g_e))):
                if c == 0:
                    sig = geno_sb[0][:, i, :].rearrange("p (n t) -> p n t", t=PACK)
                else:
                    sig = tile([P, CHUNK, PACK], F32, f"sig{c}_{i}")[:]
                nc.scalar.activation(sig, hidden[c][:].rearrange("p t n -> p n t"), ACT.Sigmoid, bias=-LN19, scale=sign)
                nc.vector.scalar_tensor_tensor(
                    ae_bf[c][:, i, :].rearrange("p (n t) -> p n t", t=PACK), sig, 1.0 / 18.0,
                    g[:, :, cols].rearrange("p t n -> p n t"), ALU.add, ALU.mult,
                )

        def quantise_ae(c):
            nc.vector.quantize_mx(out=ae_codes[c][:].bitcast(FP8X4), scales=ae_plane[c][:], in_=ae_bf[c][:].rearrange("p i w -> p (i w)"))

        def finish(first, count):
            cols = slice(first * CHUNK, (first + count) * CHUNK)
            acc = psum.tile([P, count * CHUNK], F32, name=f"rr{first}")
            for c in range(first, first + count):
                for i in range(2):
                    nc.tensor.matmul_mx(
                        out=acc[:, (c - first) * CHUNK : (c - first + 1) * CHUNK],
                        lhsT=f_codes[:, i * N : (i + 1) * N].bitcast(FP8X4),
                        lhsT_scale=f_plane[:, i * N : (i + 1) * N],
                        rhs=ae_codes[c][:, i * CHUNK : (i + 1) * CHUNK].bitcast(FP8X4),
                        rhs_scale=ae_plane[c][:, i * CHUNK : (i + 1) * CHUNK],
                        start=(i == 0),
                        stop=(i == 1),
                    )
            result = tile([P, count * CHUNK], F32, f"result{first}")
            nc.vector.tensor_tensor(result[:], acc[:], frac_sb[:, cols], ALU.mult)
            nc.sync.dma_start(out[:, cols], result[:])

        early = look_up(0, 2, "early")
        first_product(0, early[:, 0:CHUNK])
        first_product(1, early[:, CHUNK : 2 * CHUNK])
        late = look_up(2, 2, "late")
        scale_geno()
        elementwise(0)
        first_product(2, late[:, 0:CHUNK])
        elementwise(1)
        first_product(3, late[:, CHUNK : 2 * CHUNK])
        quantise_ae(0)
        quantise_ae(1)
        quantise_f()
        elementwise(2)
        elementwise(3)
        quantise_ae(2)
        quantise_ae(3)
        finish(0, 2)
        finish(2, 1)
        finish(3, 1)
